import numpy as np
import ml_dtypes

BF16 = ml_dtypes.bfloat16


def bf(x):
    return np.asarray(x, np.float32).astype(BF16)


def f32(x):
    return np.asarray(x, np.float32)


def f64(x):
    return np.asarray(x).astype(np.float64)


def striped(idx):
    return np.tile(idx.reshape(-1, 16).T, (8, 1))


S, K, M, N, E, Q = 512, 512, 256, 192, 2, 96


def gelu_tanh(v):
    return 0.5 * v * (1.0 + np.tanh(np.sqrt(2.0 / np.pi) * (v + 0.044715 * v**3)))


def setup_inputs():
    return {"base": bf(np.random.standard_normal((M, S))), "x": bf(np.random.standard_normal((K, N))), "w": bf(np.random.standard_normal((E, K, M)) / np.sqrt(K)), "b": f32(0.5 * np.random.standard_normal((M, 1))), "offs": striped(np.random.permutation(S)[:N])}


def reference(base, x, w, b, offs):
    idx = offs[:16].T.reshape(-1)
    z = f64(base).copy()
    for e in range(E):
        z[:, idx[e * Q : (e + 1) * Q]] += f64(w)[e].T @ f64(x)[:, e * Q : (e + 1) * Q]
    return gelu_tanh(z + f64(b))

@@ -1,0 +1,56 @@
+import concourse.mybir as mybir
+from concourse.masks import make_identity
+
+BF16, F32, U16 = mybir.dt.bfloat16, mybir.dt.float32, mybir.dt.uint16
+GELU_TANH = mybir.ActivationFunctionType.Gelu_apprx_tanh
+
+P = 128
+S, K, M, N, E = 512, 512, 256, 192, 2
+Q = N // E
+K_BLOCKS = K // P
+WINDOWS = M // P
+FLOPS = 2 * K * M * N
+
+
+def tile_scatter_matmul_kernel(tc, base, x, w, b, offs, out):
+    nc = tc.nc
+    with (
+        tc.tile_pool(name="held", bufs=1) as held,
+        tc.psum_pool(name="psum", bufs=1) as psum,
+    ):
+        identity = held.tile([P, P], BF16)
+        base_sb = held.tile([P, WINDOWS, S], BF16)
+        offsets = held.tile([P, N // 16], U16)
+        x_sb = held.tile([P, K_BLOCKS, N], BF16)
+        w_sb = [held.tile([P, K_BLOCKS, M], BF16, name=f"w_sb{e}") for e in range(E)]
+        bias = held.tile([P, WINDOWS], F32)
+
+        nc.sync.dma_start(base_sb[:], base.rearrange("(m p) s -> p m s", p=P))
+        nc.sync.dma_start(offsets[:], offs)
+        nc.sync.dma_start(x_sb[:], x.rearrange("(p a) n -> p a n", p=P))
+        for e in range(E):
+            nc.sync.dma_start(w_sb[e][:], w[e].rearrange("(p a) m -> p a m", p=P))
+        nc.sync.dma_start(bias[:], b.rearrange("(m p) o -> p (m o)", p=P))
+
+        make_identity(nc, identity[:])
+
+        windows = [psum.tile([P, S], F32, name=f"window{m}") for m in range(WINDOWS)]
+        for m in range(WINDOWS):
+            nc.tensor.matmul(windows[m][:], identity[:], base_sb[:, m, :], start=True, stop=False)
+
+        for e in range(E):
+            places = offsets[:, e * (Q // 16) : (e + 1) * (Q // 16)]
+            for m in range(WINDOWS):
+                for a in range(K_BLOCKS):
+                    nc.tensor.matmul(
+                        windows[m][:].indirect(places),
+                        w_sb[e][:, a, m * P : (m + 1) * P],
+                        x_sb[:, a, e * Q : (e + 1) * Q],
+                        start=False,
+                        stop=(e == E - 1 and a == K_BLOCKS - 1),
+                    )
+
+        for m in range(WINDOWS):
+            result = held.tile([P, S], F32, name=f"result{m}")
+            nc.scalar.activation(result[:], windows[m][:], GELU_TANH, bias=bias[:, m : m + 1])
+            nc.sync.dma_start(out[m * P : (m + 1) * P, :], result[:])

@@ -10,6 +10,7 @@ Q = N // E
 K_BLOCKS = K // P
 WINDOWS = M // P
 FLOPS = 2 * K * M * N
+WARM_UPS = 4
 
 
 def tile_scatter_matmul_kernel(tc, base, x, w, b, offs, out):
@@ -31,6 +32,14 @@ def tile_scatter_matmul_kernel(tc, base, x, w, b, offs, out):
         for e in range(E):
             nc.sync.dma_start(w_sb[e][:], w[e].rearrange("(p a) m -> p a m", p=P))
         nc.sync.dma_start(bias[:], b.rearrange("(m p) o -> p (m o)", p=P))
+
+        zeros = held.tile([P, S], BF16)
+        warm_bank = psum.tile([P, S], F32)
+        table_loader = held.tile([P, 1], F32)
+        nc.vector.memset(zeros[:], 0.0)
+        nc.scalar.activation(table_loader[:], zeros[:, 0:1], GELU_TANH)
+        for i in range(WARM_UPS):
+            nc.tensor.matmul(warm_bank[:], zeros[:, 0:P], zeros[:], start=True, stop=True)
 
         make_identity(nc, identity[:])
 

@@ -10,7 +10,8 @@ Q = N // E
 K_BLOCKS = K // P
 WINDOWS = M // P
 FLOPS = 2 * K * M * N
-WARM_UPS = 4
+WARM_COLUMNS = 256
+WARM_UPS = 7
 
 
 def tile_scatter_matmul_kernel(tc, base, x, w, b, offs, out):
@@ -26,15 +27,15 @@ def tile_scatter_matmul_kernel(tc, base, x, w, b, offs, out):
         w_sb = [held.tile([P, K_BLOCKS, M], BF16, name=f"w_sb{e}") for e in range(E)]
         bias = held.tile([P, WINDOWS], F32)
 
-        nc.sync.dma_start(base_sb[:], base.rearrange("(m p) s -> p m s", p=P))
+        nc.sync.dma_start(base_sb[:], base.rearrange("(p m) s -> p m s", p=P))
         nc.sync.dma_start(offsets[:], offs)
         nc.sync.dma_start(x_sb[:], x.rearrange("(p a) n -> p a n", p=P))
         for e in range(E):
             nc.sync.dma_start(w_sb[e][:], w[e].rearrange("(p a) m -> p a m", p=P))
-        nc.sync.dma_start(bias[:], b.rearrange("(m p) o -> p (m o)", p=P))
+        nc.sync.dma_start(bias[:], b.rearrange("(p m) o -> p (m o)", p=P))
 
-        zeros = held.tile([P, S], BF16)
-        warm_bank = psum.tile([P, S], F32)
+        zeros = held.tile([P, WARM_COLUMNS], BF16)
+        warm_bank = psum.tile([P, WARM_COLUMNS], F32)
         table_loader = held.tile([P, 1], F32)
         nc.vector.memset(zeros[:], 0.0)
         nc.scalar.activation(table_loader[:], zeros[:, 0:1], GELU_TANH)
@@ -53,13 +54,14 @@ def tile_scatter_matmul_kernel(tc, base, x, w, b, offs, out):
                 for a in range(K_BLOCKS):
                     nc.tensor.matmul(
                         windows[m][:].indirect(places),
-                        w_sb[e][:, a, m * P : (m + 1) * P],
+                        w_sb[e][:, a, m:M:WINDOWS],
                         x_sb[:, a, e * Q : (e + 1) * Q],
                         start=False,
                         stop=(e == E - 1 and a == K_BLOCKS - 1),
                     )
 
+        out_rows = out.rearrange("(p m) s -> p m s", p=P)
         for m in range(WINDOWS):
             result = held.tile([P, S], F32, name=f"result{m}")
             nc.scalar.activation(result[:], windows[m][:], GELU_TANH, bias=bias[:, m : m + 1])
-            nc.sync.dma_start(out[m * P : (m + 1) * P, :], result[:])
+            nc.sync.dma_start(out_rows[:, m, :], result[:])

import concourse.mybir as mybir
from concourse.masks import make_identity

BF16, F32, U16 = mybir.dt.bfloat16, mybir.dt.float32, mybir.dt.uint16
GELU_TANH = mybir.ActivationFunctionType.Gelu_apprx_tanh

P = 128
S, K, M, N, E = 512, 512, 256, 192, 2
Q = N // E
K_BLOCKS = K // P
WINDOWS = M // P
FLOPS = 2 * K * M * N
WARM_COLUMNS = 256
WARM_UPS = 7


def tile_scatter_matmul_kernel(tc, base, x, w, b, offs, out):
    nc = tc.nc
    with (
        tc.tile_pool(name="held", bufs=1) as held,
        tc.psum_pool(name="psum", bufs=1) as psum,
    ):
        identity = held.tile([P, P], BF16)
        base_sb = held.tile([P, WINDOWS, S], BF16)
        offsets = held.tile([P, N // 16], U16)
        x_sb = held.tile([P, K_BLOCKS, N], BF16)
        w_sb = [held.tile([P, K_BLOCKS, M], BF16, name=f"w_sb{e}") for e in range(E)]
        bias = held.tile([P, WINDOWS], F32)

        nc.sync.dma_start(base_sb[:], base.rearrange("(p m) s -> p m s", p=P))
        nc.sync.dma_start(offsets[:], offs)
        nc.sync.dma_start(x_sb[:], x.rearrange("(p a) n -> p a n", p=P))
        for e in range(E):
            nc.sync.dma_start(w_sb[e][:], w[e].rearrange("(p a) m -> p a m", p=P))
        nc.sync.dma_start(bias[:], b.rearrange("(p m) o -> p (m o)", p=P))

        zeros = held.tile([P, WARM_COLUMNS], BF16)
        warm_bank = psum.tile([P, WARM_COLUMNS], F32)
        table_loader = held.tile([P, 1], F32)
        nc.vector.memset(zeros[:], 0.0)
        nc.scalar.activation(table_loader[:], zeros[:, 0:1], GELU_TANH)
        for i in range(WARM_UPS):
            nc.tensor.matmul(warm_bank[:], zeros[:, 0:P], zeros[:], start=True, stop=True)

        make_identity(nc, identity[:])

        windows = [psum.tile([P, S], F32, name=f"window{m}") for m in range(WINDOWS)]
        for m in range(WINDOWS):
            nc.tensor.matmul(windows[m][:], identity[:], base_sb[:, m, :], start=True, stop=False)

        for e in range(E):
            places = offsets[:, e * (Q // 16) : (e + 1) * (Q // 16)]
            for m in range(WINDOWS):
                for a in range(K_BLOCKS):
                    nc.tensor.matmul(
                        windows[m][:].indirect(places),
                        w_sb[e][:, a, m:M:WINDOWS],
                        x_sb[:, a, e * Q : (e + 1) * Q],
                        start=False,
                        stop=(e == E - 1 and a == K_BLOCKS - 1),
                    )

        out_rows = out.rearrange("(p m) s -> p m s", p=P)
        for m in range(WINDOWS):
            result = held.tile([P, S], F32, name=f"result{m}")
            nc.scalar.activation(result[:], windows[m][:], GELU_TANH, bias=bias[:, m : m + 1])
            nc.sync.dma_start(out_rows[:, m, :], result[:])
